import numpy as np
import ml_dtypes


def mxq(x, axis, fmt="e4m3"):
    dtype, down = {"e4m3": (ml_dtypes.float8_e4m3fn, 7), "e5m2": (ml_dtypes.float8_e5m2, 14)}[fmt]
    v = np.moveaxis(np.asarray(x, np.float32).astype(ml_dtypes.bfloat16).astype(np.float64), axis, -1)
    blocks = v.reshape(v.shape[:-1] + (-1, 32))
    amax = np.abs(blocks).max(-1, keepdims=True)
    byte = np.maximum(np.where(amax > 0, np.frexp(amax)[1] - 1 + 127, 0) - down, 1)
    scale = np.exp2(byte - 127.0)
    codes = (blocks / scale).astype(np.float32).astype(dtype).astype(np.float64)
    return np.moveaxis((codes * scale).reshape(v.shape), -1, axis)


WIDE = False


def mx_kscale(k):
    if not WIDE:
        return np.ones(k)
    levels = np.array([10, -10, 5, -5, 0])
    if k % 512:
        return np.exp2(np.random.permutation(np.resize(levels, k // 32))).repeat(32)
    a = np.empty((k // 512, 16))
    for p in range(k // 512):
        a[p, :8] = np.random.permutation(np.resize(levels, 8))
        for g in range(8):
            far = levels[np.abs(levels - a[p, g]) >= 10]
            a[p, g + 8] = far[np.random.randint(len(far))]
    return np.exp2(a.ravel()).repeat(32)


def f64(x):
    return np.asarray(x).astype(np.float64)


def striped(idx):
    return np.tile(idx.reshape(-1, 16).T, (8, 1)).astype(np.uint16)


def unstriped(offs):
    return offs[:16].T.reshape(-1).astype(np.int64)


def striped8(idx):
    return np.concatenate([x.reshape(-1, 16).T for x in idx]).astype(np.uint16)


def runs(offs, k):
    lists = np.stack([offs[16 * r : 16 * r + 16].T.reshape(-1) for r in range(8)]).astype(np.int64)
    return lists[np.arange(k) % 512 // 64]


def pack_weight(w):
    k, n = w.shape
    w = f64(np.asarray(w, np.float32).astype(ml_dtypes.bfloat16)).reshape(k // 32, 32, n)
    amax = np.abs(w).max(1)
    byte = np.clip(np.where(amax > 0, np.frexp(amax)[1] - 1 + 127 - 7, 1), 1, 254)
    scaled = (w * np.exp2(127.0 - byte)[:, None, :]).reshape(k, n).astype(np.float32)
    words = np.ascontiguousarray(scaled.reshape(k // 512, 128, 4, n).transpose(0, 1, 3, 2)).astype(ml_dtypes.float8_e4m3fn).view(np.uint8)
    return words, np.ascontiguousarray(byte.astype(np.uint8).reshape(k // 512, 16, n))


def unpack_weight(words, scales):
    g, p, n, _ = words.shape
    vals = np.ascontiguousarray(words).view(ml_dtypes.float8_e4m3fn).astype(np.float64) * np.repeat(np.exp2(scales.astype(np.float64) - 127.0), 8, axis=1)[..., None]
    return vals.transpose(0, 1, 3, 2).reshape(g * 512, n)


K, T, S, H, W, C = 512, 2048, 256, 512, 1024, 512


def setup_inputs():
    n = np.random.standard_normal
    s = mx_kscale(K)[:, None]
    packed_xT = pack_weight(n((K, T)) * s)
    return {
        "x_words": packed_xT[0],
        "x_scales": packed_xT[1],
        "w1": (n((K, H)) / np.sqrt(K) / s).astype(np.float32),
        "gs": (np.random.uniform(0.5, 1.5, (K, 1)) / s).astype(np.float32),
        "wb": (n((K, S)) / np.sqrt(K) / s).astype(np.float32),
        "offs": striped(np.random.permutation(T)[:S]),
        "n1": striped(np.random.randint(0, S, W)),
        "cand": striped(np.random.permutation(T)[:C]),
        "cb": striped(np.random.permutation(T)[:C]),
        "n2": striped8(np.stack([np.random.permutation(S) for _ in range(8)])),
        "n3": striped8(np.stack([np.random.permutation(S) for _ in range(8)])),
        "n4": striped8(np.stack([np.random.permutation(S) for _ in range(8)])),
    }


def reference(x_words, x_scales, w1, gs, wb, offs, n1, cand, cb, n2, n3, n4):
    x_cand = unpack_weight(x_words, x_scales)[:, unstriped(cand)]
    xq = unpack_weight(x_words, x_scales)[:, unstriped(offs)]
    y = mxq(f64(w1), 0, "e4m3").T @ xq
    mb = y[:, unstriped(n1)]
    mn = mb.reshape(H, S, 4).min(axis=2)
    mx = mb.reshape(H, S, 4).max(axis=2)
    z = f64(gs) * (np.maximum(y, mn) - (0.5 * mx))
    a = 0.0625 * ((x_cand.T @ mxq(z, 0, "e4m3")))
    x_cb = unpack_weight(x_words, x_scales)[:, unstriped(cb)]
    b = x_cb.T @ mxq(f64(wb), 0, "e4m3")
    return np.maximum(np.minimum(a - (0.5 * (a[np.arange(C)[:, None], runs(n2, C)])), b[np.arange(C)[:, None], runs(n3, C)]), b[np.arange(C)[:, None], runs(n4, C)])

@@ -1,0 +1,198 @@
+from contextlib import ExitStack
+
+import concourse.mybir as mybir
+
+F32 = mybir.dt.float32
+BF16 = mybir.dt.bfloat16
+I32 = mybir.dt.int32
+U32 = mybir.dt.uint32
+U16 = mybir.dt.uint16
+U8 = mybir.dt.uint8
+FP8X4 = mybir.dt.float8_e4m3fn_x4
+ALU = mybir.AluOpType
+COPY = mybir.ActivationFunctionType.Copy
+
+P = 128
+K, T, S, H, W, C = 512, 2048, 256, 512, 1024, 512
+FLOPS = 2 * K * H * S + 2 * 2 * K * C * S
+Y_WIN = 528
+AB_WIN = 512
+
+
+def tile_picked_cdswclampbgmid_none_p_kernel(
+    tc, x_words, x_scales, w1, gs, wb, offs, n1, cand, cb, n2, n3, n4, out
+):
+    nc = tc.nc
+    with ExitStack() as ctx:
+        lists = ctx.enter_context(tc.tile_pool(name="lists", bufs=1))
+        keep = ctx.enter_context(tc.tile_pool(name="keep", bufs=1))
+        ring = ctx.enter_context(tc.tile_pool(name="ring", bufs=4))
+        psum = ctx.enter_context(tc.psum_pool(name="psum", bufs=1))
+
+        def load_list(name, src):
+            tile = lists.tile(list(src.shape), U16, name=name)
+            nc.sync.dma_start(tile[:], src)
+            return tile
+
+        xs = keep.tile([P, T], U8, name="xs", align_bytes=64)
+        nc.vector.memset(xs[:].bitcast(I32), 0)
+        offs_t = load_list("offs_t", offs)
+        cb_t = load_list("cb_t", cb)
+        w1_rows = w1.rearrange("(p j) c -> p j c", j=4)
+        w1_raw = []
+        for h in range(2):
+            raw = keep.tile([P, 4, 256], F32, name="w1_raw%d" % h)
+            nc.sync.dma_start(raw[:], w1_rows[:, :, 256 * h : 256 * (h + 1)])
+            w1_raw.append(raw)
+        for q in range(4):
+            nc.scalar.dma_start(
+                xs[32 * q : 32 * q + 4, :].bitcast(I32), x_scales[0, 4 * q : 4 * q + 4, :].bitcast(I32)
+            )
+        xw = keep.tile([P, T], U32, name="xw", align_bytes=64)
+        nc.sync.dma_start(xw[:].bitcast(I32), x_words[0].rearrange("p n t -> p (n t)").bitcast(I32))
+        cand_t = load_list("cand_t", cand)
+        wb_raw = keep.tile([P, 4, S], F32, name="wb_raw")
+        nc.sync.dma_start(wb_raw[:], wb.rearrange("(p j) c -> p j c", j=4))
+        n1_t = load_list("n1_t", n1)
+        n3_t = load_list("n3_t", n3)
+        n4_t = load_list("n4_t", n4)
+        n2_t = load_list("n2_t", n2)
+        gs_t = keep.tile([P, 4], F32, name="gs_t")
+        nc.gpsimd.dma_start(gs_t[:], gs.rearrange("(p t) o -> p (t o)", t=4))
+
+        y_win = [keep.tile([P, Y_WIN], F32, name="y_win%d" % t) for t in range(4)]
+        b_win = [keep.tile([P, AB_WIN], F32, name="b_win%d" % t) for t in range(4)]
+        a_win = y_win
+        for win in y_win + b_win:
+            nc.vector.memset(win[:, S:], 0.0)
+
+        w1_g = keep.tile([P, 4, P, 4], BF16, name="w1_g", align_bytes=64)
+        for h in range(2):
+            nc.scalar.copy(
+                w1_g[:, :, 64 * h : 64 * (h + 1), :].rearrange("p t m j -> p m t j"),
+                w1_raw[h][:].rearrange("p j (m t) -> p m t j", t=4),
+            )
+
+        def gather_scales(name, lst, n):
+            tile = keep.tile([P, n], U8, name=name, align_bytes=64)
+            nc.vector.tensor_copy(tile[:], xs[:].indirect(lst[:]))
+            return tile
+
+        def dealt_scales(name, lst):
+            plain = gather_scales(name + "_plain", lst, C)
+            tile = keep.tile([P, 4, P], U8, name=name, align_bytes=64)
+            nc.vector.tensor_copy(
+                tile[:].rearrange("p t (c i) -> p c t i", i=16),
+                plain[:].rearrange("p (c i t) -> p c t i", i=16, t=4),
+            )
+            return tile
+
+        def dealt_words(name, lst):
+            tile = keep.tile([P, 4, P], U32, name=name, align_bytes=64)
+            nc.vector.tensor_copy(tile[:].rearrange("p t m -> p m t"), xw[:].indirect(lst[:]))
+            return tile
+
+        xq_s = gather_scales("xq_s", offs_t, S)
+        cb_s = dealt_scales("cb_s", cb_t)
+        w1_c = keep.tile([P, H], U32, name="w1_c", align_bytes=64)
+        w1_s = keep.tile([P, H], U8, name="w1_s", align_bytes=64)
+        nc.vector.quantize_mx(
+            out=w1_c[:].bitcast(FP8X4), scales=w1_s[:], in_=w1_g[:].rearrange("p t m j -> p (t m j)")
+        )
+        xq_w = keep.tile([P, S], U32, name="xq_w", align_bytes=64)
+        nc.vector.tensor_copy(xq_w[:], xw[:].indirect(offs_t[:]))
+        cand_s = dealt_scales("cand_s", cand_t)
+
+        def product(tag, words, scales, rhs_words, rhs_scales):
+            acc = psum.tile([P, S], F32, name=tag, tag=tag)
+            nc.tensor.matmul_mx(
+                out=acc[:],
+                lhsT=words.bitcast(FP8X4),
+                lhsT_scale=scales,
+                rhs=rhs_words[:].bitcast(FP8X4),
+                rhs_scale=rhs_scales[:],
+                start=True,
+                stop=True,
+            )
+            return acc
+
+        y_acc = [
+            product("ya%d" % t, w1_c[:, P * t : P * (t + 1)], w1_s[:, P * t : P * (t + 1)], xq_w, xq_s)
+            for t in range(4)
+        ]
+
+        cb_w = dealt_words("cb_w", cb_t)
+        wb_g = keep.tile([P, S, 4], BF16, name="wb_g", align_bytes=64)
+        nc.vector.tensor_copy(
+            wb_g[:].rearrange("p (c i) j -> p c j i", i=4),
+            wb_raw[:].rearrange("p j (c i) -> p c j i", i=4),
+        )
+        cand_w = dealt_words("cand_w", cand_t)
+        wb_c = keep.tile([P, S], U32, name="wb_c", align_bytes=64)
+        wb_s = keep.tile([P, S], U8, name="wb_s", align_bytes=64)
+        nc.vector.quantize_mx(
+            out=wb_c[:].bitcast(FP8X4), scales=wb_s[:], in_=wb_g[:].rearrange("p c j -> p (c j)")
+        )
+        b_acc = [product("b%d" % t, cb_w[:, t, :], cb_s[:, t, :], wb_c, wb_s) for t in range(4)]
+
+        v = keep.tile([P, 4, S], F32, name="v")
+        for t in range(4):
+            nc.scalar.copy(y_win[t][:, :S], y_acc[t][:])
+            lo = ring.tile([P, S, 2], F32, name="lo")
+            hi = ring.tile([P, S, 2], F32, name="hi")
+            for h in range(2):
+                mb = ring.tile([P, P, 4], F32, name="mb")
+                nc.scalar.activation(
+                    mb[:].rearrange("p j m -> p (j m)"),
+                    y_win[t][:].indirect(n1_t[:, 32 * h : 32 * (h + 1)]),
+                    COPY,
+                )
+                cols = slice(P * h, P * (h + 1))
+                nc.vector.tensor_tensor(lo[:, cols, :], mb[:, :, 0:2], mb[:, :, 2:4], ALU.min)
+                nc.vector.tensor_tensor(hi[:, cols, :], mb[:, :, 0:2], mb[:, :, 2:4], ALU.max)
+            mn = ring.tile([P, S], F32, name="mn")
+            mx = ring.tile([P, S], F32, name="mx")
+            u = ring.tile([P, S], F32, name="u")
+            nc.vector.tensor_tensor(mn[:], lo[:, :, 0], lo[:, :, 1], ALU.min)
+            nc.vector.tensor_tensor(mx[:], hi[:, :, 0], hi[:, :, 1], ALU.max)
+            nc.vector.tensor_tensor(u[:], y_win[t][:, :S], mn[:], ALU.max)
+            nc.vector.scalar_tensor_tensor(v[:, t, :], mx[:], -0.5, u[:], ALU.mult, ALU.add)
+
+        z_g = keep.tile([P, S, 4], BF16, name="z_g", align_bytes=64)
+        z_c = keep.tile([P, S], U32, name="z_c", align_bytes=64)
+        z_s = keep.tile([P, S], U8, name="z_s", align_bytes=64)
+        gs_b = gs_t[:].unsqueeze(1).unsqueeze(3).broadcast_to([P, 32, 4, 4])
+        for h in range(2):
+            cols = slice(P * h, P * (h + 1))
+            nc.vector.tensor_tensor(
+                z_g[:, cols, :].rearrange("p (c i) t -> p c t i", i=4),
+                v[:, :, cols].rearrange("p t (c i) -> p c t i", i=4),
+                gs_b,
+                ALU.mult,
+            )
+        for h in range(2):
+            cols = slice(P * h, P * (h + 1))
+            nc.vector.quantize_mx(
+                out=z_c[:, cols].bitcast(FP8X4),
+                scales=z_s[:, cols],
+                in_=z_g[:, cols, :].rearrange("p c t -> p (c t)"),
+            )
+        a_acc = [product("ya%d" % t, cand_w[:, t, :], cand_s[:, t, :], z_c, z_s) for t in range(4)]
+
+        out_rows = out.rearrange("(p t) j -> p t j", t=4)
+        for t in range(4):
+            nc.scalar.copy(b_win[t][:, :S], b_acc[t][:])
+            g3 = ring.tile([P, S], F32, name="g3")
+            g4 = ring.tile([P, S], F32, name="g4")
+            g2 = ring.tile([P, S], F32, name="g2")
+            nc.scalar.activation(g3[:], b_win[t][:].indirect(n3_t[:]), COPY)
+            nc.scalar.activation(g4[:], b_win[t][:].indirect(n4_t[:]), COPY)
+            nc.vector.tensor_scalar(a_win[t][:, :S], a_acc[t][:], 0.0625, None, ALU.mult)
+            nc.scalar.activation(g2[:], a_win[t][:].indirect(n2_t[:]), COPY)
+            d = ring.tile([P, S], F32, name="d")
+            e = ring.tile([P, S], F32, name="e")
+            o = ring.tile([P, S], F32, name="o")
+            nc.vector.scalar_tensor_tensor(d[:], g2[:], -0.5, a_win[t][:, :S], ALU.mult, ALU.add)
+            nc.vector.tensor_tensor(e[:], d[:], g3[:], ALU.min)
+            nc.vector.tensor_tensor(o[:], e[:], g4[:], ALU.max)
+            nc.sync.dma_start(out_rows[:, t, :], o[:])

@@ -27,6 +27,7 @@ def tile_picked_cdswclampbgmid_none_p_kernel(
         lists = ctx.enter_context(tc.tile_pool(name="lists", bufs=1))
         keep = ctx.enter_context(tc.tile_pool(name="keep", bufs=1))
         ring = ctx.enter_context(tc.tile_pool(name="ring", bufs=4))
+        shared = ctx.enter_context(tc.tile_pool(name="shared", bufs=1))
         psum = ctx.enter_context(tc.psum_pool(name="psum", bufs=1))
 
         def load_list(name, src):
@@ -38,131 +39,110 @@ def tile_picked_cdswclampbgmid_none_p_kernel(
         nc.vector.memset(xs[:].bitcast(I32), 0)
         offs_t = load_list("offs_t", offs)
         cb_t = load_list("cb_t", cb)
+        cand_t = load_list("cand_t", cand)
+        for q in range(4):
+            nc.scalar.dma_start(
+                xs[32 * q : 32 * q + 4, :].bitcast(I32), x_scales[0, 4 * q : 4 * q + 4, :].bitcast(I32)
+            )
         w1_rows = w1.rearrange("(p j) c -> p j c", j=4)
         w1_raw = []
         for h in range(2):
             raw = keep.tile([P, 4, 256], F32, name="w1_raw%d" % h)
             nc.sync.dma_start(raw[:], w1_rows[:, :, 256 * h : 256 * (h + 1)])
             w1_raw.append(raw)
-        for q in range(4):
-            nc.scalar.dma_start(
-                xs[32 * q : 32 * q + 4, :].bitcast(I32), x_scales[0, 4 * q : 4 * q + 4, :].bitcast(I32)
-            )
         xw = keep.tile([P, T], U32, name="xw", align_bytes=64)
         nc.sync.dma_start(xw[:].bitcast(I32), x_words[0].rearrange("p n t -> p (n t)").bitcast(I32))
-        cand_t = load_list("cand_t", cand)
-        wb_raw = keep.tile([P, 4, S], F32, name="wb_raw")
-        nc.sync.dma_start(wb_raw[:], wb.rearrange("(p j) c -> p j c", j=4))
         n1_t = load_list("n1_t", n1)
         n3_t = load_list("n3_t", n3)
         n4_t = load_list("n4_t", n4)
         n2_t = load_list("n2_t", n2)
         gs_t = keep.tile([P, 4], F32, name="gs_t")
-        nc.gpsimd.dma_start(gs_t[:], gs.rearrange("(p t) o -> p (t o)", t=4))
+        nc.sync.dma_start(gs_t[:], gs.rearrange("(p t) o -> p (t o)", t=4))
 
         y_win = [keep.tile([P, Y_WIN], F32, name="y_win%d" % t) for t in range(4)]
         b_win = [keep.tile([P, AB_WIN], F32, name="b_win%d" % t) for t in range(4)]
-        a_win = y_win
-        for win in y_win + b_win:
+        a_win = [keep.tile([P, AB_WIN], F32, name="a_win%d" % t) for t in range(4)]
+        for win in y_win + b_win + a_win:
             nc.vector.memset(win[:, S:], 0.0)
 
-        w1_g = keep.tile([P, 4, P, 4], BF16, name="w1_g", align_bytes=64)
+        w1_g = shared.tile([P, 4, P, 4], BF16, name="w1_g", align_bytes=64, offset=0)
         for h in range(2):
             nc.scalar.copy(
                 w1_g[:, :, 64 * h : 64 * (h + 1), :].rearrange("p t m j -> p m t j"),
                 w1_raw[h][:].rearrange("p j (m t) -> p m t j", t=4),
             )
 
-        def gather_scales(name, lst, n):
-            tile = keep.tile([P, n], U8, name=name, align_bytes=64)
-            nc.vector.tensor_copy(tile[:], xs[:].indirect(lst[:]))
-            return tile
-
-        def dealt_scales(name, lst):
-            plain = gather_scales(name + "_plain", lst, C)
+        def dealt_scales(name, lst, offset):
+            plain = shared.tile([P, C], U8, name=name + "_plain", align_bytes=64, offset=offset)
+            nc.vector.tensor_copy(plain[:], xs[:].indirect(lst[:]))
             tile = keep.tile([P, 4, P], U8, name=name, align_bytes=64)
             nc.vector.tensor_copy(
-                tile[:].rearrange("p t (c i) -> p c t i", i=16),
-                plain[:].rearrange("p (c i t) -> p c t i", i=16, t=4),
+                tile[:].bitcast(I32).rearrange("p t (g w) -> p g t w", w=4),
+                plain[:].bitcast(I32).rearrange("p (g t w) -> p g t w", t=4, w=4),
             )
             return tile
 
-        def dealt_words(name, lst):
-            tile = keep.tile([P, 4, P], U32, name=name, align_bytes=64)
-            nc.vector.tensor_copy(tile[:].rearrange("p t m -> p m t"), xw[:].indirect(lst[:]))
+        def dealt_words(name, lst, offset):
+            tile = shared.tile([P, 4, P], U32, name=name, align_bytes=64, offset=offset)
+            nc.vector.tensor_copy(tile[:].rearrange("p t (g r) -> p g t r", r=16), xw[:].indirect(lst[:]))
             return tile
 
-        xq_s = gather_scales("xq_s", offs_t, S)
-        cb_s = dealt_scales("cb_s", cb_t)
+        xq_s = keep.tile([P, S], U8, name="xq_s", align_bytes=64)
+        nc.vector.tensor_copy(xq_s[:], xs[:].indirect(offs_t[:]))
+        cb_s = dealt_scales("cb_s", cb_t, 4096)
         w1_c = keep.tile([P, H], U32, name="w1_c", align_bytes=64)
         w1_s = keep.tile([P, H], U8, name="w1_s", align_bytes=64)
         nc.vector.quantize_mx(
             out=w1_c[:].bitcast(FP8X4), scales=w1_s[:], in_=w1_g[:].rearrange("p t m j -> p (t m j)")
         )
-        xq_w = keep.tile([P, S], U32, name="xq_w", align_bytes=64)
+        xq_w = shared.tile([P, S], U32, name="xq_w", align_bytes=64, offset=8704)
         nc.vector.tensor_copy(xq_w[:], xw[:].indirect(offs_t[:]))
-        cand_s = dealt_scales("cand_s", cand_t)
+        cand_s = dealt_scales("cand_s", cand_t, 8192)
 
-        def product(tag, words, scales, rhs_words, rhs_scales):
-            acc = psum.tile([P, S], F32, name=tag, tag=tag)
+        def product(acc, words, scales, rhs_words, rhs_scales):
             nc.tensor.matmul_mx(
-                out=acc[:],
+                out=acc,
                 lhsT=words.bitcast(FP8X4),
                 lhsT_scale=scales,
-                rhs=rhs_words[:].bitcast(FP8X4),
-                rhs_scale=rhs_scales[:],
+                rhs=rhs_words.bitcast(FP8X4),
+                rhs_scale=rhs_scales,
                 start=True,
                 stop=True,
             )
-            return acc
 
-        y_acc = [
-            product("ya%d" % t, w1_c[:, P * t : P * (t + 1)], w1_s[:, P * t : P * (t + 1)], xq_w, xq_s)
-            for t in range(4)
-        ]
+        y_acc = [psum.tile([P, 2, S], F32, name="y_acc%d" % i) for i in range(2)]
+        b_acc = [psum.tile([P, 2, S], F32, name="b_acc%d" % i) for i in range(2)]
+        a_acc = [psum.tile([P, S], F32, name="a_acc%d" % t) for t in range(4)]
+        for t in range(4):
+            cols = slice(P * t, P * (t + 1))
+            product(y_acc[t // 2][:, t % 2, :], w1_c[:, cols], w1_s[:, cols], xq_w[:], xq_s[:])
 
-        cb_w = dealt_words("cb_w", cb_t)
+        nc.scalar.copy(y_win[0][:, :S], y_acc[0][:, 0, :])
+        cb_w = dealt_words("cb_w", cb_t, 0)
+        for t in range(1, 4):
+            nc.vector.tensor_copy(y_win[t][:, :S], y_acc[t // 2][:, t % 2, :])
+        wb_raw = shared.tile([P, 4, S], F32, name="wb_raw", align_bytes=64, offset=4096)
+        nc.sync.dma_start(wb_raw[:], wb.rearrange("(p j) c -> p j c", j=4))
         wb_g = keep.tile([P, S, 4], BF16, name="wb_g", align_bytes=64)
-        nc.vector.tensor_copy(
-            wb_g[:].rearrange("p (c i) j -> p c j i", i=4),
-            wb_raw[:].rearrange("p j (c i) -> p c j i", i=4),
-        )
-        cand_w = dealt_words("cand_w", cand_t)
+        nc.gpsimd.tensor_scalar(wb_g[:], wb_raw[:].rearrange("p j c -> p c j"), 1.0, 0.0, ALU.mult, ALU.add)
+        cand_w = dealt_words("cand_w", cand_t, 8704)
         wb_c = keep.tile([P, S], U32, name="wb_c", align_bytes=64)
         wb_s = keep.tile([P, S], U8, name="wb_s", align_bytes=64)
-        nc.vector.quantize_mx(
-            out=wb_c[:].bitcast(FP8X4), scales=wb_s[:], in_=wb_g[:].rearrange("p c j -> p (c j)")
-        )
-        b_acc = [product("b%d" % t, cb_w[:, t, :], cb_s[:, t, :], wb_c, wb_s) for t in range(4)]
+
+        def b_product():
+            nc.vector.quantize_mx(
+                out=wb_c[:].bitcast(FP8X4), scales=wb_s[:], in_=wb_g[:].rearrange("p c j -> p (c j)")
+            )
+            for t in range(4):
+                product(b_acc[t // 2][:, t % 2, :], cb_w[:, t, :], cb_s[:, t, :], wb_c[:], wb_s[:])
 
         v = keep.tile([P, 4, S], F32, name="v")
-        for t in range(4):
-            nc.scalar.copy(y_win[t][:, :S], y_acc[t][:])
-            lo = ring.tile([P, S, 2], F32, name="lo")
-            hi = ring.tile([P, S, 2], F32, name="hi")
-            for h in range(2):
-                mb = ring.tile([P, P, 4], F32, name="mb")
-                nc.scalar.activation(
-                    mb[:].rearrange("p j m -> p (j m)"),
-                    y_win[t][:].indirect(n1_t[:, 32 * h : 32 * (h + 1)]),
-                    COPY,
-                )
-                cols = slice(P * h, P * (h + 1))
-                nc.vector.tensor_tensor(lo[:, cols, :], mb[:, :, 0:2], mb[:, :, 2:4], ALU.min)
-                nc.vector.tensor_tensor(hi[:, cols, :], mb[:, :, 0:2], mb[:, :, 2:4], ALU.max)
-            mn = ring.tile([P, S], F32, name="mn")
-            mx = ring.tile([P, S], F32, name="mx")
-            u = ring.tile([P, S], F32, name="u")
-            nc.vector.tensor_tensor(mn[:], lo[:, :, 0], lo[:, :, 1], ALU.min)
-            nc.vector.tensor_tensor(mx[:], hi[:, :, 0], hi[:, :, 1], ALU.max)
-            nc.vector.tensor_tensor(u[:], y_win[t][:, :S], mn[:], ALU.max)
-            nc.vector.scalar_tensor_tensor(v[:, t, :], mx[:], -0.5, u[:], ALU.mult, ALU.add)
-
         z_g = keep.tile([P, S, 4], BF16, name="z_g", align_bytes=64)
         z_c = keep.tile([P, S], U32, name="z_c", align_bytes=64)
         z_s = keep.tile([P, S], U8, name="z_s", align_bytes=64)
         gs_b = gs_t[:].unsqueeze(1).unsqueeze(3).broadcast_to([P, 32, 4, 4])
-        for h in range(2):
+
+        def z_weight(h):
             cols = slice(P * h, P * (h + 1))
             nc.vector.tensor_tensor(
                 z_g[:, cols, :].rearrange("p (c i) t -> p c t i", i=4),
@@ -170,29 +150,91 @@ def tile_picked_cdswclampbgmid_none_p_kernel(
                 gs_b,
                 ALU.mult,
             )
-        for h in range(2):
+
+        def z_product(h):
             cols = slice(P * h, P * (h + 1))
             nc.vector.quantize_mx(
                 out=z_c[:, cols].bitcast(FP8X4),
                 scales=z_s[:, cols],
                 in_=z_g[:, cols, :].rearrange("p c t -> p (c t)"),
             )
-        a_acc = [product("ya%d" % t, cand_w[:, t, :], cand_s[:, t, :], z_c, z_s) for t in range(4)]
+            for t in range(4):
+                product(a_acc[t][:, cols], cand_w[:, t, :], cand_s[:, t, :], z_c[:, cols], z_s[:, cols])
 
-        out_rows = out.rearrange("(p t) j -> p t j", t=4)
+        def larger(step):
+            h, i, mn, mx, u = step
+            nc.vector.tensor_tensor(u[:], y_acc[i][:, :, P * h : P * (h + 1)], mn[:], ALU.max)
+
+        def less_half(step):
+            h, i, mn, mx, u = step
+            nc.vector.scalar_tensor_tensor(
+                v[:, 2 * i : 2 * i + 2, P * h : P * (h + 1)], mx[:], -0.5, u[:], ALU.mult, ALU.add
+            )
+
+        last = None
+        for h in range(2):
+            for i in range(2):
+                lo = ring.tile([P, 2, P, 2], F32, name="lo")
+                hi = ring.tile([P, 2, P, 2], F32, name="hi")
+                mn = ring.tile([P, 2, P], F32, name="mn")
+                mx = ring.tile([P, 2, P], F32, name="mx")
+                u = ring.tile([P, 2, P], F32, name="u")
+                for k in range(2):
+                    t = 2 * i + k
+                    mb = keep.tile([P, P, 4], F32, name="mb%d%d" % (h, t))
+                    nc.scalar.activation(
+                        mb[:].rearrange("p j m -> p (j m)"),
+                        y_win[t][:].indirect(n1_t[:, 32 * h : 32 * (h + 1)]),
+                        COPY,
+                    )
+                    nc.vector.tensor_tensor(lo[:, k], mb[:, :, 0:2], mb[:, :, 2:4], ALU.min)
+                    if last and k == 0:
+                        larger(last)
+                    nc.vector.tensor_tensor(hi[:, k], mb[:, :, 0:2], mb[:, :, 2:4], ALU.max)
+                    if last and k == 0:
+                        less_half(last)
+                    if (h, i, k) == (1, 1, 0):
+                        z_product(0)
+                nc.vector.tensor_tensor(mn[:], lo[:, :, :, 0], lo[:, :, :, 1], ALU.min)
+                nc.vector.tensor_tensor(mx[:], hi[:, :, :, 0], hi[:, :, :, 1], ALU.max)
+                if (h, i) == (0, 0):
+                    b_product()
+                if (h, i) == (1, 0):
+                    z_weight(0)
+                last = (h, i, mn, mx, u)
+        larger(last)
+        less_half(last)
+        z_weight(1)
+        z_product(1)
+
+        out_rows = out.rearrange("(g t r) j -> t g r j", t=4, r=16)
+        g3 = [keep.tile([P, S], F32, name="g3_%d" % t) for t in range(4)]
+        g4 = [keep.tile([P, S], F32, name="g4_%d" % t) for t in range(4)]
+        g2 = [keep.tile([P, S], F32, name="g2_%d" % t) for t in range(4)]
+
+        def fetch_b(t):
+            nc.scalar.copy(b_win[t][:, :S], b_acc[t // 2][:, t % 2, :])
+            nc.scalar.activation(g3[t][:], b_win[t][:].indirect(n3_t[:]), COPY)
+            nc.scalar.activation(g4[t][:], b_win[t][:].indirect(n4_t[:]), COPY)
+
         for t in range(4):
-            nc.scalar.copy(b_win[t][:, :S], b_acc[t][:])
-            g3 = ring.tile([P, S], F32, name="g3")
-            g4 = ring.tile([P, S], F32, name="g4")
-            g2 = ring.tile([P, S], F32, name="g2")
-            nc.scalar.activation(g3[:], b_win[t][:].indirect(n3_t[:]), COPY)
-            nc.scalar.activation(g4[:], b_win[t][:].indirect(n4_t[:]), COPY)
+            fetch_b(t)
+        for t in range(2):
             nc.vector.tensor_scalar(a_win[t][:, :S], a_acc[t][:], 0.0625, None, ALU.mult)
-            nc.scalar.activation(g2[:], a_win[t][:].indirect(n2_t[:]), COPY)
+        for t in range(4):
+            if t >= 2:
+                nc.scalar.activation(a_win[t][:, :S], a_acc[t][:], COPY, scale=0.0625)
+            width = S if t < 3 else P
+            parts = [slice(c, c + width) for c in range(0, S, width)]
             d = ring.tile([P, S], F32, name="d")
             e = ring.tile([P, S], F32, name="e")
             o = ring.tile([P, S], F32, name="o")
-            nc.vector.scalar_tensor_tensor(d[:], g2[:], -0.5, a_win[t][:, :S], ALU.mult, ALU.add)
-            nc.vector.tensor_tensor(e[:], d[:], g3[:], ALU.min)
-            nc.vector.tensor_tensor(o[:], e[:], g4[:], ALU.max)
-            nc.sync.dma_start(out_rows[:, t, :], o[:])
+            for c in parts:
+                nc.scalar.activation(g2[t][:, c], a_win[t][:].indirect(n2_t[:, c.start // 16 : c.stop // 16]), COPY)
+            for c in parts:
+                nc.vector.scalar_tensor_tensor(d[:, c], g2[t][:, c], -0.5, a_win[t][:, c], ALU.mult, ALU.add)
+            for c in parts:
+                nc.vector.tensor_tensor(e[:, c], d[:, c], g3[t][:, c], ALU.min)
+            for c in parts:
+                nc.vector.tensor_tensor(o[:, c], e[:, c], g4[t][:, c], ALU.max)
+                nc.sync.dma_start(out_rows[t, :, :, c], o[:, c])

from contextlib import ExitStack

import concourse.mybir as mybir

F32 = mybir.dt.float32
BF16 = mybir.dt.bfloat16
I32 = mybir.dt.int32
U32 = mybir.dt.uint32
U16 = mybir.dt.uint16
U8 = mybir.dt.uint8
FP8X4 = mybir.dt.float8_e4m3fn_x4
ALU = mybir.AluOpType
COPY = mybir.ActivationFunctionType.Copy

P = 128
K, T, S, H, W, C = 512, 2048, 256, 512, 1024, 512
FLOPS = 2 * K * H * S + 2 * 2 * K * C * S
Y_WIN = 528
AB_WIN = 512


def tile_picked_cdswclampbgmid_none_p_kernel(
    tc, x_words, x_scales, w1, gs, wb, offs, n1, cand, cb, n2, n3, n4, out
):
    nc = tc.nc
    with ExitStack() as ctx:
        lists = ctx.enter_context(tc.tile_pool(name="lists", bufs=1))
        keep = ctx.enter_context(tc.tile_pool(name="keep", bufs=1))
        ring = ctx.enter_context(tc.tile_pool(name="ring", bufs=4))
        shared = ctx.enter_context(tc.tile_pool(name="shared", bufs=1))
        psum = ctx.enter_context(tc.psum_pool(name="psum", bufs=1))

        def load_list(name, src):
            tile = lists.tile(list(src.shape), U16, name=name)
            nc.sync.dma_start(tile[:], src)
            return tile

        xs = keep.tile([P, T], U8, name="xs", align_bytes=64)
        nc.vector.memset(xs[:].bitcast(I32), 0)
        offs_t = load_list("offs_t", offs)
        cb_t = load_list("cb_t", cb)
        cand_t = load_list("cand_t", cand)
        for q in range(4):
            nc.scalar.dma_start(
                xs[32 * q : 32 * q + 4, :].bitcast(I32), x_scales[0, 4 * q : 4 * q + 4, :].bitcast(I32)
            )
        w1_rows = w1.rearrange("(p j) c -> p j c", j=4)
        w1_raw = []
        for h in range(2):
            raw = keep.tile([P, 4, 256], F32, name="w1_raw%d" % h)
            nc.sync.dma_start(raw[:], w1_rows[:, :, 256 * h : 256 * (h + 1)])
            w1_raw.append(raw)
        xw = keep.tile([P, T], U32, name="xw", align_bytes=64)
        nc.sync.dma_start(xw[:].bitcast(I32), x_words[0].rearrange("p n t -> p (n t)").bitcast(I32))
        n1_t = load_list("n1_t", n1)
        n3_t = load_list("n3_t", n3)
        n4_t = load_list("n4_t", n4)
        n2_t = load_list("n2_t", n2)
        gs_t = keep.tile([P, 4], F32, name="gs_t")
        nc.sync.dma_start(gs_t[:], gs.rearrange("(p t) o -> p (t o)", t=4))

        y_win = [keep.tile([P, Y_WIN], F32, name="y_win%d" % t) for t in range(4)]
        b_win = [keep.tile([P, AB_WIN], F32, name="b_win%d" % t) for t in range(4)]
        a_win = [keep.tile([P, AB_WIN], F32, name="a_win%d" % t) for t in range(4)]
        for win in y_win + b_win + a_win:
            nc.vector.memset(win[:, S:], 0.0)

        w1_g = shared.tile([P, 4, P, 4], BF16, name="w1_g", align_bytes=64, offset=0)
        for h in range(2):
            nc.scalar.copy(
                w1_g[:, :, 64 * h : 64 * (h + 1), :].rearrange("p t m j -> p m t j"),
                w1_raw[h][:].rearrange("p j (m t) -> p m t j", t=4),
            )

        def dealt_scales(name, lst, offset):
            plain = shared.tile([P, C], U8, name=name + "_plain", align_bytes=64, offset=offset)
            nc.vector.tensor_copy(plain[:], xs[:].indirect(lst[:]))
            tile = keep.tile([P, 4, P], U8, name=name, align_bytes=64)
            nc.vector.tensor_copy(
                tile[:].bitcast(I32).rearrange("p t (g w) -> p g t w", w=4),
                plain[:].bitcast(I32).rearrange("p (g t w) -> p g t w", t=4, w=4),
            )
            return tile

        def dealt_words(name, lst, offset):
            tile = shared.tile([P, 4, P], U32, name=name, align_bytes=64, offset=offset)
            nc.vector.tensor_copy(tile[:].rearrange("p t (g r) -> p g t r", r=16), xw[:].indirect(lst[:]))
            return tile

        xq_s = keep.tile([P, S], U8, name="xq_s", align_bytes=64)
        nc.vector.tensor_copy(xq_s[:], xs[:].indirect(offs_t[:]))
        cb_s = dealt_scales("cb_s", cb_t, 4096)
        w1_c = keep.tile([P, H], U32, name="w1_c", align_bytes=64)
        w1_s = keep.tile([P, H], U8, name="w1_s", align_bytes=64)
        nc.vector.quantize_mx(
            out=w1_c[:].bitcast(FP8X4), scales=w1_s[:], in_=w1_g[:].rearrange("p t m j -> p (t m j)")
        )
        xq_w = shared.tile([P, S], U32, name="xq_w", align_bytes=64, offset=8704)
        nc.vector.tensor_copy(xq_w[:], xw[:].indirect(offs_t[:]))
        cand_s = dealt_scales("cand_s", cand_t, 8192)

        def product(acc, words, scales, rhs_words, rhs_scales):
            nc.tensor.matmul_mx(
                out=acc,
                lhsT=words.bitcast(FP8X4),
                lhsT_scale=scales,
                rhs=rhs_words.bitcast(FP8X4),
                rhs_scale=rhs_scales,
                start=True,
                stop=True,
            )

        y_acc = [psum.tile([P, 2, S], F32, name="y_acc%d" % i) for i in range(2)]
        b_acc = [psum.tile([P, 2, S], F32, name="b_acc%d" % i) for i in range(2)]
        a_acc = [psum.tile([P, S], F32, name="a_acc%d" % t) for t in range(4)]
        for t in range(4):
            cols = slice(P * t, P * (t + 1))
            product(y_acc[t // 2][:, t % 2, :], w1_c[:, cols], w1_s[:, cols], xq_w[:], xq_s[:])

        nc.scalar.copy(y_win[0][:, :S], y_acc[0][:, 0, :])
        cb_w = dealt_words("cb_w", cb_t, 0)
        for t in range(1, 4):
            nc.vector.tensor_copy(y_win[t][:, :S], y_acc[t // 2][:, t % 2, :])
        wb_raw = shared.tile([P, 4, S], F32, name="wb_raw", align_bytes=64, offset=4096)
        nc.sync.dma_start(wb_raw[:], wb.rearrange("(p j) c -> p j c", j=4))
        wb_g = keep.tile([P, S, 4], BF16, name="wb_g", align_bytes=64)
        nc.gpsimd.tensor_scalar(wb_g[:], wb_raw[:].rearrange("p j c -> p c j"), 1.0, 0.0, ALU.mult, ALU.add)
        cand_w = dealt_words("cand_w", cand_t, 8704)
        wb_c = keep.tile([P, S], U32, name="wb_c", align_bytes=64)
        wb_s = keep.tile([P, S], U8, name="wb_s", align_bytes=64)

        def b_product():
            nc.vector.quantize_mx(
                out=wb_c[:].bitcast(FP8X4), scales=wb_s[:], in_=wb_g[:].rearrange("p c j -> p (c j)")
            )
            for t in range(4):
                product(b_acc[t // 2][:, t % 2, :], cb_w[:, t, :], cb_s[:, t, :], wb_c[:], wb_s[:])

        v = keep.tile([P, 4, S], F32, name="v")
        z_g = keep.tile([P, S, 4], BF16, name="z_g", align_bytes=64)
        z_c = keep.tile([P, S], U32, name="z_c", align_bytes=64)
        z_s = keep.tile([P, S], U8, name="z_s", align_bytes=64)
        gs_b = gs_t[:].unsqueeze(1).unsqueeze(3).broadcast_to([P, 32, 4, 4])

        def z_weight(h):
            cols = slice(P * h, P * (h + 1))
            nc.vector.tensor_tensor(
                z_g[:, cols, :].rearrange("p (c i) t -> p c t i", i=4),
                v[:, :, cols].rearrange("p t (c i) -> p c t i", i=4),
                gs_b,
                ALU.mult,
            )

        def z_product(h):
            cols = slice(P * h, P * (h + 1))
            nc.vector.quantize_mx(
                out=z_c[:, cols].bitcast(FP8X4),
                scales=z_s[:, cols],
                in_=z_g[:, cols, :].rearrange("p c t -> p (c t)"),
            )
            for t in range(4):
                product(a_acc[t][:, cols], cand_w[:, t, :], cand_s[:, t, :], z_c[:, cols], z_s[:, cols])

        def larger(step):
            h, i, mn, mx, u = step
            nc.vector.tensor_tensor(u[:], y_acc[i][:, :, P * h : P * (h + 1)], mn[:], ALU.max)

        def less_half(step):
            h, i, mn, mx, u = step
            nc.vector.scalar_tensor_tensor(
                v[:, 2 * i : 2 * i + 2, P * h : P * (h + 1)], mx[:], -0.5, u[:], ALU.mult, ALU.add
            )

        last = None
        for h in range(2):
            for i in range(2):
                lo = ring.tile([P, 2, P, 2], F32, name="lo")
                hi = ring.tile([P, 2, P, 2], F32, name="hi")
                mn = ring.tile([P, 2, P], F32, name="mn")
                mx = ring.tile([P, 2, P], F32, name="mx")
                u = ring.tile([P, 2, P], F32, name="u")
                for k in range(2):
                    t = 2 * i + k
                    mb = keep.tile([P, P, 4], F32, name="mb%d%d" % (h, t))
                    nc.scalar.activation(
                        mb[:].rearrange("p j m -> p (j m)"),
                        y_win[t][:].indirect(n1_t[:, 32 * h : 32 * (h + 1)]),
                        COPY,
                    )
                    nc.vector.tensor_tensor(lo[:, k], mb[:, :, 0:2], mb[:, :, 2:4], ALU.min)
                    if last and k == 0:
                        larger(last)
                    nc.vector.tensor_tensor(hi[:, k], mb[:, :, 0:2], mb[:, :, 2:4], ALU.max)
                    if last and k == 0:
                        less_half(last)
                    if (h, i, k) == (1, 1, 0):
                        z_product(0)
                nc.vector.tensor_tensor(mn[:], lo[:, :, :, 0], lo[:, :, :, 1], ALU.min)
                nc.vector.tensor_tensor(mx[:], hi[:, :, :, 0], hi[:, :, :, 1], ALU.max)
                if (h, i) == (0, 0):
                    b_product()
                if (h, i) == (1, 0):
                    z_weight(0)
                last = (h, i, mn, mx, u)
        larger(last)
        less_half(last)
        z_weight(1)
        z_product(1)

        out_rows = out.rearrange("(g t r) j -> t g r j", t=4, r=16)
        g3 = [keep.tile([P, S], F32, name="g3_%d" % t) for t in range(4)]
        g4 = [keep.tile([P, S], F32, name="g4_%d" % t) for t in range(4)]
        g2 = [keep.tile([P, S], F32, name="g2_%d" % t) for t in range(4)]

        def fetch_b(t):
            nc.scalar.copy(b_win[t][:, :S], b_acc[t // 2][:, t % 2, :])
            nc.scalar.activation(g3[t][:], b_win[t][:].indirect(n3_t[:]), COPY)
            nc.scalar.activation(g4[t][:], b_win[t][:].indirect(n4_t[:]), COPY)

        for t in range(4):
            fetch_b(t)
        for t in range(2):
            nc.vector.tensor_scalar(a_win[t][:, :S], a_acc[t][:], 0.0625, None, ALU.mult)
        for t in range(4):
            if t >= 2:
                nc.scalar.activation(a_win[t][:, :S], a_acc[t][:], COPY, scale=0.0625)
            width = S if t < 3 else P
            parts = [slice(c, c + width) for c in range(0, S, width)]
            d = ring.tile([P, S], F32, name="d")
            e = ring.tile([P, S], F32, name="e")
            o = ring.tile([P, S], F32, name="o")
            for c in parts:
                nc.scalar.activation(g2[t][:, c], a_win[t][:].indirect(n2_t[:, c.start // 16 : c.stop // 16]), COPY)
            for c in parts:
                nc.vector.scalar_tensor_tensor(d[:, c], g2[t][:, c], -0.5, a_win[t][:, c], ALU.mult, ALU.add)
            for c in parts:
                nc.vector.tensor_tensor(e[:, c], d[:, c], g3[t][:, c], ALU.min)
            for c in parts:
                nc.vector.tensor_tensor(o[:, c], e[:, c], g4[t][:, c], ALU.max)
                nc.sync.dma_start(out_rows[t, :, :, c], o[:, c])
